import numpy as np
import ml_dtypes


def mxq(x, axis, fmt="e4m3"):
    dtype, down = {"e4m3": (ml_dtypes.float8_e4m3fn, 7), "e5m2": (ml_dtypes.float8_e5m2, 14)}[fmt]
    v = np.moveaxis(np.asarray(x, np.float32).astype(ml_dtypes.bfloat16).astype(np.float64), axis, -1)
    blocks = v.reshape(v.shape[:-1] + (-1, 32))
    amax = np.abs(blocks).max(-1, keepdims=True)
    byte = np.maximum(np.where(amax > 0, np.frexp(amax)[1] - 1 + 127, 0) - down, 1)
    scale = np.exp2(byte - 127.0)
    codes = (blocks / scale).astype(np.float32).astype(dtype).astype(np.float64)
    return np.moveaxis((codes * scale).reshape(v.shape), -1, axis)


WIDE = False


def mx_kscale(k):
    if not WIDE:
        return np.ones(k)
    levels = np.array([10, -10, 5, -5, 0])
    if k % 512:
        return np.exp2(np.random.permutation(np.resize(levels, k // 32))).repeat(32)
    a = np.empty((k // 512, 16))
    for p in range(k // 512):
        a[p, :8] = np.random.permutation(np.resize(levels, 8))
        for g in range(8):
            far = levels[np.abs(levels - a[p, g]) >= 10]
            a[p, g + 8] = far[np.random.randint(len(far))]
    return np.exp2(a.ravel()).repeat(32)


BF16 = ml_dtypes.bfloat16


def bf(x):
    return np.asarray(x, np.float32).astype(BF16)


def f64(x):
    return np.asarray(x).astype(np.float64)


E2M1 = np.array([0.0, 0.5, 1.0, 1.5, 2.0, 3.0, 4.0, 6.0, -0.0, -0.5, -1.0, -1.5, -2.0, -3.0, -4.0, -6.0])


def pack_weight(w, fmt):
    k, n = w.shape
    w = f64(bf(w)).reshape(k // 32, 32, n)
    amax = np.abs(w).max(1)
    if fmt == "e4m3":
        byte = np.frexp(amax)[1] - 1 + 127 - 7
    else:
        mant, ex = np.frexp(amax / 6.0)
        byte = np.where(mant > 0.5, ex, ex - 1) + 127
    byte = np.clip(np.where(amax > 0, byte, 1), 1, 254)
    scaled = (w * np.exp2(127.0 - byte)[:, None, :]).reshape(k, n).astype(np.float32)
    by_word = np.ascontiguousarray(scaled.reshape(k // 512, 128, 4, n).transpose(0, 1, 3, 2))
    if fmt == "e4m3":
        words = by_word.astype(ml_dtypes.float8_e4m3fn).view(np.uint8)
    else:
        c = by_word.astype(ml_dtypes.float4_e2m1fn).view(np.uint8) & 0xF
        words = c[..., 0::2] | (c[..., 1::2] << 4)
    return np.ascontiguousarray(words), np.ascontiguousarray(byte.astype(np.uint8).reshape(k // 512, 16, n))


def unpack_weight(words, scales, fmt):
    g, p, n, _ = words.shape
    if fmt == "e4m3":
        vals = np.ascontiguousarray(words).view(ml_dtypes.float8_e4m3fn).astype(np.float64)
    else:
        nib = np.empty((g, p, n, 4), np.uint8)
        nib[..., 0::2] = words & 0xF
        nib[..., 1::2] = words >> 4
        vals = E2M1[nib]
    vals = vals * np.repeat(np.exp2(scales.astype(np.float64) - 127.0), 8, axis=1)[..., None]
    return vals.transpose(0, 1, 3, 2).reshape(g * 512, n)

def planes(Y):
    n, m = Y.shape
    b = f64(bf(Y)).reshape(n // 32, 32, m)
    amax = np.abs(b).max(1)
    byte = np.clip(np.where(amax > 0, np.frexp(amax)[1] - 1 + 127 - 7, 1), 1, 254)
    codes = (b * np.exp2(127.0 - byte)[:, None, :]).reshape(n, m).astype(np.float32).astype(ml_dtypes.float8_e4m3fn).view(np.uint8)
    words = codes.reshape(n // 512, 128, 4, m).transpose(0, 1, 3, 2)
    return np.ascontiguousarray(words), np.ascontiguousarray(byte.astype(np.uint8).reshape(n // 512, 16, m))


B, D, H, C = 1024, 1024, 1024, 512


def setup_inputs():
    s, t = mx_kscale(D), mx_kscale(H)
    x = bf(np.random.standard_normal((B, D)) * s)
    w1_words, w1_scales = pack_weight(np.random.standard_normal((D, H)) * 1.2 / np.sqrt(D) / s[:, None], "e4m3")
    g1 = bf((1.0 + 0.1 * np.random.standard_normal(H)) * t)
    v1_words, v1_scales = pack_weight(np.random.standard_normal((H, C)) / np.sqrt(H) / t[:, None], "e4m3")
    wx_words, wx_scales = pack_weight(np.random.standard_normal((D, C)) * 0.8 / np.sqrt(D) / s[:, None], "e4m3")
    wh_words, wh_scales = pack_weight(np.random.standard_normal((H, C)) * 1.2 / np.sqrt(H) / t[:, None], "e4m3")
    u = bf(np.random.standard_normal((B, C)))
    return {
        "x": x,
        "w1_words": w1_words,
        "w1_scales": w1_scales,
        "g1": g1,
        "v1_words": v1_words,
        "v1_scales": v1_scales,
        "wx_words": wx_words,
        "wx_scales": wx_scales,
        "wh_words": wh_words,
        "wh_scales": wh_scales,
        "u": u,
    }


def centred_features(xq, w1_words, w1_scales, g1):
    r = np.maximum(xq @ unpack_weight(w1_words, w1_scales, "e4m3"), 0.0)
    return (r - np.mean(r, axis=0, keepdims=True)) * f64(g1)[None, :]


def newton_target(y, score):
    return y * (1.0 + np.exp(-y * score))


def core(x, w1_words, w1_scales, g1, v1_words, v1_scales, wx_words, wx_scales, wh_words, wh_scales, u):
    xq = mxq(f64(x), 1, "e4m3")
    h = centred_features(xq, w1_words, w1_scales, g1)
    hq = mxq(h, 1, "e4m3")
    s1 = hq @ unpack_weight(v1_words, v1_scales, "e4m3")
    p = (xq @ unpack_weight(wx_words, wx_scales, "e4m3")) + (hq @ unpack_weight(wh_words, wh_scales, "e4m3"))
    score = 0.8 * s1 + 0.8 * np.tanh(p)
    y = np.where(f64(u) < 0, -1.0, 1.0)
    return newton_target(y, score)


def reference(x, w1_words, w1_scales, g1, v1_words, v1_scales, wx_words, wx_scales, wh_words, wh_scales, u):
    R_out = core(x, w1_words, w1_scales, g1, v1_words, v1_scales, wx_words, wx_scales, wh_words, wh_scales, u)
    words, scales = planes(R_out)
    return R_out, words, scales

@@ -1,0 +1,361 @@
+from contextlib import ExitStack
+
+import concourse.mybir as mybir
+from concourse.masks import make_identity
+
+F32 = mybir.dt.float32
+BF16 = mybir.dt.bfloat16
+I32 = mybir.dt.int32
+U8 = mybir.dt.uint8
+FP8X4 = mybir.dt.float8_e4m3fn_x4
+ALU = mybir.AluOpType
+ACT = mybir.ActivationFunctionType
+
+B, D, H, C = 1024, 1024, 1024, 512
+P = 128
+FLOPS = 2 * B * D * H + 3 * 2 * B * D * C
+LN2 = 0.6931471805599453
+
+
+def tile_grownetnewtontargets_x2_kernel(
+    tc, x, w1_words, w1_scales, g1, v1_words, v1_scales, wx_words, wx_scales, wh_words, wh_scales, u, out_0, out_1, out_2
+):
+    nc = tc.nc
+    with ExitStack() as ctx:
+        keep = ctx.enter_context(tc.tile_pool(name="keep", bufs=1))
+        work = ctx.enter_context(tc.tile_pool(name="work", bufs=4))
+        psum = ctx.enter_context(tc.psum_pool(name="psum", bufs=8))
+
+        ident = keep.tile([P, P], F32, name="ident")
+        w1s = keep.tile([P, 1024], U8, name="w1s", align_bytes=64)
+        w1sp = keep.tile([P, 8, 128], U8, name="w1sp", align_bytes=64)
+        ws = keep.tile([P, 3, 512], U8, name="ws", align_bytes=64)
+        x_sb = keep.tile([P, 8, 1024], BF16, name="x_sb", align_bytes=64)
+        xg = keep.tile([P, 2, 2, 512, 4], BF16, name="xg", align_bytes=64)
+        xq = keep.tile([P, 2, 1024], I32, name="xq", align_bytes=64)
+        xs = keep.tile([P, 2, 1024], U8, name="xs", align_bytes=64)
+        w1w = keep.tile([P, 2, 2, 512], I32, name="w1w", align_bytes=64)
+        w1p = keep.tile([P, 2, 8, 128], I32, name="w1p", align_bytes=64)
+        ww = keep.tile([P, 3, 2, 512], I32, name="ww", align_bytes=64)
+        u_sb = keep.tile([P, 8, 512], BF16, name="u_sb", align_bytes=64)
+        hy = keep.tile([P, 8, 512], BF16, name="hy", align_bytes=64)
+        g1b = keep.tile([P, 2, 4], BF16, name="g1b", align_bytes=64)
+        g1f = keep.tile([P, 8], F32, name="g1f", align_bytes=64)
+        zero = keep.tile([P, 1], F32, name="zero")
+        ln2 = keep.tile([P, 1], F32, name="ln2")
+        warm = keep.tile([P, 1], F32, name="warm")
+        sums = keep.tile([P, 8, 2], F32, name="sums", align_bytes=64)
+        mean = keep.tile([P, 8], F32, name="mean", align_bytes=64)
+        nmg = keep.tile([P, 8], F32, name="nmg", align_bytes=64)
+        r = keep.tile([P, 8, 1024], F32, name="r", align_bytes=64)
+        hc = keep.tile([P, 2, 4, 1024], BF16, name="hc", align_bytes=64)
+        hg = keep.tile([P, 2, 2, 512, 4], BF16, name="hg", align_bytes=64)
+        hq = keep.tile([P, 2, 1024], I32, name="hq", align_bytes=64)
+        hs = keep.tile([P, 2, 1024], U8, name="hs", align_bytes=64)
+        o = keep.tile([P, 2, 4, 512], F32, name="o", align_bytes=64)
+        pb = keep.tile([P, 2, 512, 4], BF16, name="pb", align_bytes=64)
+        pq = keep.tile([P, 2, 512], I32, name="pq", align_bytes=64)
+        ps0 = keep.tile([P, 512], U8, name="ps0", align_bytes=64)
+        ps1 = keep.tile([P, 512], U8, name="ps1", align_bytes=64)
+        ps = [ps0, ps1]
+
+        ctx.enter_context(tc.manual_schedule())
+        nc.vector.memset(w1s[:].bitcast(I32), 0)
+        nc.vector.memset(zero[:], 0.0)
+        nc.vector.memset(ws[:].rearrange("p w n -> p (w n)").bitcast(I32), 0)
+        make_identity(nc, ident[:])
+        nc.vector.tensor_scalar(out=ln2[:], in0=zero[:], scalar1=1.0, scalar2=LN2, op0=ALU.mult, op1=ALU.add)
+
+        xv = x.rearrange("(g p t) k -> g p t k", p=P, t=4)
+        w1v = w1_words.rearrange("g p n t -> p g (n t)").bitcast(I32)
+        uv = u.rearrange("(g p t) c -> g p t c", p=P, t=4)
+        for q in range(4):
+            nc.scalar.dma_start(
+                out=w1s[32 * q : 32 * q + 8, :].bitcast(I32), in_=w1_scales[:, 4 * q : 4 * q + 4, :].bitcast(I32)
+            )
+        nc.scalar.activation(out=warm[:], in_=zero[:], func=ACT.Exp)
+        nc.gpsimd.dma_start(out=g1b[:], in_=g1.rearrange("(g p t) -> p g t", p=P, t=4))
+        for g in range(2):
+            for t in range(4):
+                nc.sync.dma_start(out=x_sb[:, 4 * g + t, :], in_=xv[g][:, t, :])
+            nc.sync.dma_start(out=w1w[:, g, :, :], in_=w1v[:, :, 512 * g : 512 * g + 512])
+        for g in range(2):
+            nc.sync.dma_start(out=u_sb[:, 4 * g : 4 * g + 4, :], in_=uv[g])
+        for i, s in enumerate((wx_scales, v1_scales, wh_scales)):
+            for q in range(4):
+                nc.sync.dma_start(
+                    out=ws[32 * q : 32 * q + 8, i, :].bitcast(I32), in_=s[:, 4 * q : 4 * q + 4, :].bitcast(I32)
+                )
+        for i, w in ((0, wx_words), (2, wh_words), (1, v1_words)):
+            nc.sync.dma_start(out=ww[:, i, :, :], in_=w.rearrange("g p n t -> p g (n t)").bitcast(I32))
+
+        def turn(j):
+            xw = x_sb[:, j, :].bitcast(F32)
+            xt = psum.tile([P, 4, P], F32, name="bank")
+            for k in range(2):
+                for e in range(2):
+                    nc.tensor.transpose(xt[:, 2 * k + e, :], xw[:, 256 * k + e : 256 * (k + 1) : 2], ident[:])
+            return xt
+
+        def lay(eng, j, xt):
+            g, t = j // 4, j % 4
+            out = xg[:, g, :, 128 * t : 128 * t + 128, :].bitcast(F32)
+            src = xt[:].rearrange("p (k e) n -> p k n e", k=2)
+            if eng == "v":
+                nc.vector.tensor_copy(out=out, in_=src)
+            else:
+                nc.scalar.copy(out=out, in_=src)
+
+        def quant_x(g, half):
+            for k in range(2):
+                c = slice(512 * g + 256 * half, 512 * g + 256 * half + 256)
+                nc.vector.quantize_mx(
+                    out=xq[:, k, c].bitcast(FP8X4),
+                    scales=xs[:, k, c],
+                    in_=xg[:, g, k, 256 * half : 256 * half + 256, :].rearrange("p n t -> p (n t)"),
+                )
+
+        def order_w1(gh):
+            nc.vector.tensor_copy(
+                out=w1p[:, :, 4 * gh : 4 * gh + 4, :], in_=w1w[:, gh, :, :].rearrange("p k (m t) -> p k t m", t=4)
+            )
+
+        def stage1(eng, ht, g):
+            acc = psum.tile([P, 512], F32, name="bank")
+            for k in range(2):
+                nc.tensor.matmul_mx(
+                    out=acc[:],
+                    lhsT=w1p[:, k, ht, :].bitcast(FP8X4),
+                    lhsT_scale=w1sp[4 * k :, ht, :],
+                    rhs=xq[:, k, 512 * g : 512 * g + 512].bitcast(FP8X4),
+                    rhs_scale=xs[:, k, 512 * g : 512 * g + 512],
+                    start=(k == 0),
+                    stop=(k == 1),
+                )
+            out = r[:, ht, 512 * g : 512 * g + 512]
+            if eng == "v":
+                nc.vector.tensor_scalar(
+                    out=out, in0=acc[:], scalar1=0.0, scalar2=None, op0=ALU.max, op1=ALU.add, accum_out=sums[:, ht, g : g + 1]
+                )
+            else:
+                nc.scalar.activation(out=out, in_=acc[:], func=ACT.Relu, accum_out=sums[:, ht, g : g + 1])
+            if g == 1:
+                nc.gpsimd.tensor_scalar(
+                    out=mean[:, ht : ht + 1],
+                    in0=sums[:, ht, 0:1],
+                    scalar1=sums[:, ht, 1:2],
+                    scalar2=1.0 / B,
+                    op0=ALU.add,
+                    op1=ALU.mult,
+                )
+
+        def centre(eng, ht):
+            gh, t = ht // 4, ht % 4
+            if eng == "v":
+                nc.vector.tensor_scalar(
+                    out=hc[:, gh, t, :],
+                    in0=r[:, ht, :],
+                    scalar1=mean[:, ht : ht + 1],
+                    scalar2=g1f[:, ht : ht + 1],
+                    op0=ALU.subtract,
+                    op1=ALU.mult,
+                )
+            else:
+                nc.gpsimd.tensor_scalar(
+                    out=nmg[:, ht : ht + 1],
+                    in0=mean[:, ht : ht + 1],
+                    scalar1=-1.0,
+                    scalar2=g1f[:, ht : ht + 1],
+                    op0=ALU.mult,
+                    op1=ALU.mult,
+                )
+                nc.scalar.activation(
+                    out=hc[:, gh, t, :],
+                    in_=r[:, ht, :],
+                    func=ACT.Identity,
+                    scale=g1f[:, ht : ht + 1],
+                    bias=nmg[:, ht : ht + 1],
+                )
+
+        def interleave(eng, gh, g, lo=0, hi=512):
+            src = hc[:, gh, :, 512 * g + lo : 512 * g + hi].rearrange("p t n -> p n t")
+            if eng == "v":
+                nc.vector.tensor_copy(out=hg[:, gh, g, lo:hi, :], in_=src)
+            else:
+                nc.scalar.copy(out=hg[:, gh, g, lo:hi, :], in_=src)
+
+        def quant_h(gh, g):
+            nc.vector.quantize_mx(
+                out=hq[:, gh, 512 * g : 512 * g + 512].bitcast(FP8X4),
+                scales=hs[:, gh, 512 * g : 512 * g + 512],
+                in_=hg[:, gh, g, :, :].rearrange("p n t -> p (n t)"),
+            )
+
+        def signs(g):
+            nc.vector.tensor_scalar(
+                out=hy[:, 4 * g : 4 * g + 4, :],
+                in0=u_sb[:, 4 * g : 4 * g + 4, :],
+                scalar1=0.0,
+                scalar2=0.5,
+                op0=ALU.is_ge,
+                op1=ALU.subtract,
+            )
+
+        def passes(acc, codes, scales, j, wi, first, last):
+            for k in range(2):
+                nc.tensor.matmul_mx(
+                    out=acc[:],
+                    lhsT=codes[:, k, P * j : P * j + P].bitcast(FP8X4),
+                    lhsT_scale=scales[:, k, P * j : P * j + P],
+                    rhs=ww[:, wi, k, :].bitcast(FP8X4),
+                    rhs_scale=ws[4 * k :, wi, :],
+                    start=(first and k == 0),
+                    stop=(last and k == 1),
+                )
+
+        pbank, sbank, ths, qs, e1s, e2s = {}, {}, {}, {}, {}, {}
+
+        def open_p(j):
+            acc = psum.tile([P, 512], F32, name="bank")
+            passes(acc, xq, xs, j, 0, True, False)
+            pbank[j] = acc
+
+        def close_p(j):
+            passes(pbank[j], hq, hs, j, 2, False, True)
+
+        def open_s(j):
+            acc = psum.tile([P, 512], F32, name="bank")
+            passes(acc, hq, hs, j, 1, True, True)
+            sbank[j] = acc
+
+        def tanh(j):
+            th = work.tile([P, 512], F32, name="th")
+            nc.scalar.activation(out=th[:], in_=pbank[j][:], func=ACT.Tanh)
+            ths[j] = th
+
+        def add(j):
+            q = work.tile([P, 512], F32, name="q")
+            nc.vector.tensor_tensor(out=q[:], in0=sbank[j][:], in1=ths[j][:], op=ALU.add)
+            qs[j] = q
+
+        def sign(j):
+            e1 = work.tile([P, 512], F32, name="e1")
+            nc.vector.tensor_tensor(out=e1[:], in0=qs[j][:], in1=hy[:, j, :], op=ALU.mult)
+            e1s[j] = e1
+
+        def expo(j):
+            e2 = work.tile([P, 512], F32, name="e2")
+            nc.scalar.activation(out=e2[:], in_=e1s[j][:], func=ACT.Exp, bias=ln2[:], scale=-1.6)
+            e2s[j] = e2
+
+        o0v = out_0.rearrange("(g p t) c -> g p t c", p=P, t=4)
+
+        def final(j, lo=0, hi=512):
+            g, t = j // 4, j % 4
+            nc.vector.scalar_tensor_tensor(
+                out=o[:, g, t, lo:hi], in0=e2s[j][:, lo:hi], scalar=2.0, in1=hy[:, j, lo:hi], op0=ALU.add, op1=ALU.mult
+            )
+            if hi == 512:
+                nc.sync.dma_start(out=o0v[g][:, t, :], in_=o[:, g, t, :])
+
+        def weave(eng, g, lo, hi):
+            src = o[:, g, :, lo:hi].rearrange("p t c -> p c t")
+            if eng == "v":
+                nc.vector.tensor_copy(out=pb[:, g, lo:hi, :], in_=src)
+            else:
+                nc.scalar.copy(out=pb[:, g, lo:hi, :], in_=src)
+
+        def planes(g):
+            nc.vector.quantize_mx(
+                out=pq[:, g, :].bitcast(FP8X4), scales=ps[g][:], in_=pb[:, g, :, :].rearrange("p c t -> p (c t)")
+            )
+            nc.sync.dma_start(out=out_1[g].rearrange("p m t -> p (m t)").bitcast(I32), in_=pq[:, g, :])
+            for qd in range(4):
+                nc.sync.dma_start(
+                    out=out_2[g][4 * qd : 4 * qd + 4, :].bitcast(I32), in_=ps[g][32 * qd : 32 * qd + 4, :].bitcast(I32)
+                )
+
+        nc.vector.tensor_copy(
+            out=w1sp[:].rearrange("p (g t) m -> p g t m", g=2), in_=w1s[:].rearrange("p (g m t) -> p g t m", g=2, t=4)
+        )
+        for j in range(4):
+            lay("s", j, turn(j))
+            if j == 1:
+                quant_x(0, 0)
+        order_w1(0)
+        quant_x(0, 1)
+        for j in range(4, 8):
+            lay("s", j, turn(j))
+            if j == 5:
+                quant_x(1, 0)
+        quant_x(1, 1)
+        for ht in range(4):
+            stage1("v" if ht == 2 else "s", ht, 0)
+        order_w1(1)
+        nc.vector.tensor_copy(out=g1f[:], in_=g1b[:].rearrange("p g t -> p (g t)"))
+        signs(0)
+        signs(1)
+        for ht in range(4):
+            stage1("s", ht, 1)
+        centre("v", 0)
+        centre("v", 1)
+        centre("v", 2)
+        stage1("s", 4, 0)
+        stage1("v", 4, 1)
+        centre("v", 3)
+        stage1("s", 5, 0)
+        stage1("s", 5, 1)
+        interleave("v", 0, 0)
+        quant_h(0, 0)
+        stage1("v", 6, 0)
+        stage1("s", 6, 1)
+        stage1("s", 7, 0)
+        stage1("s", 7, 1)
+        centre("v", 5)
+        centre("s", 4)
+        centre("v", 6)
+        centre("s", 7)
+        interleave("v", 0, 1, 256, 512)
+        interleave("v", 1, 0, 0, 320)
+        interleave("s", 1, 0, 320, 512)
+        quant_h(1, 0)
+        interleave("s", 0, 1, 0, 256)
+        quant_h(0, 1)
+        interleave("v", 1, 1, 256, 512)
+        interleave("s", 1, 1, 0, 256)
+        for j in range(6):
+            open_p(j)
+        for j in range(4):
+            close_p(j)
+            open_s(j)
+            if j in (1, 2):
+                open_p(j + 5)
+        tanh(0)
+        tanh(1)
+        for j in range(10):
+            if 1 <= j < 7:
+                tanh(j + 1)
+            if j < 8:
+                add(j)
+            if j == 1:
+                quant_h(1, 1)
+                for i in range(4, 8):
+                    close_p(i)
+                    open_s(i)
+            if j >= 2:
+                if j == 9:
+                    final(7, 0, 256)
+                    final(7, 256, 512)
+                else:
+                    final(j - 2)
+            if j < 8:
+                sign(j)
+                expo(j)
+            if 5 <= j < 8:
+                weave("s", 0, 128 * (j - 5), 128 * (j - 4))
+            if j == 8:
+                weave("v", 0, 384, 512)
+        weave("s", 1, 0, 192)
+        planes(0)
+        weave("v", 1, 192, 512)
+        planes(1)

@@ -61,6 +61,8 @@ def tile_grownetnewtontargets_x2_kernel(
 
         ctx.enter_context(tc.manual_schedule())
         nc.vector.memset(w1s[:].bitcast(I32), 0)
+        blank = keep.tile([P, 512], BF16, name="blank", align_bytes=64)
+        nc.vector.memset(blank[:], 0.0)
         nc.vector.memset(zero[:], 0.0)
         nc.vector.memset(ws[:].rearrange("p w n -> p (w n)").bitcast(I32), 0)
         make_identity(nc, ident[:])
@@ -69,21 +71,24 @@ def tile_grownetnewtontargets_x2_kernel(
         xv = x.rearrange("(g p t) k -> g p t k", p=P, t=4)
         w1v = w1_words.rearrange("g p n t -> p g (n t)").bitcast(I32)
         uv = u.rearrange("(g p t) c -> g p t c", p=P, t=4)
-        for q in range(4):
-            nc.scalar.dma_start(
-                out=w1s[32 * q : 32 * q + 8, :].bitcast(I32), in_=w1_scales[:, 4 * q : 4 * q + 4, :].bitcast(I32)
-            )
         nc.scalar.activation(out=warm[:], in_=zero[:], func=ACT.Exp)
         nc.gpsimd.dma_start(out=g1b[:], in_=g1.rearrange("(g p t) -> p g t", p=P, t=4))
-        for g in range(2):
-            for t in range(4):
-                nc.sync.dma_start(out=x_sb[:, 4 * g + t, :], in_=xv[g][:, t, :])
-            nc.sync.dma_start(out=w1w[:, g, :, :], in_=w1v[:, :, 512 * g : 512 * g + 512])
+        nc.sync.dma_start(out=x_sb[:, 0, :], in_=xv[0][:, 0, :])
+        for q in range(4):
+            nc.sync.dma_start(
+                out=w1s[32 * q : 32 * q + 8, :].bitcast(I32), in_=w1_scales[:, 4 * q : 4 * q + 4, :].bitcast(I32)
+            )
+        nc.sync.dma_start(out=x_sb[:, 1, :], in_=xv[0][:, 1, :])
+        nc.sync.dma_start(out=x_sb[:, 2:4, :], in_=xv[0][:, 2:4, :])
+        nc.sync.dma_start(out=w1w[:, 0, :, :], in_=w1v[:, :, 0:512])
+        nc.sync.dma_start(out=x_sb[:, 4:6, :], in_=xv[1][:, 0:2, :])
+        nc.sync.dma_start(out=x_sb[:, 6:8, :], in_=xv[1][:, 2:4, :])
+        nc.sync.dma_start(out=w1w[:, 1, :, :], in_=w1v[:, :, 512:1024])
         for g in range(2):
             nc.sync.dma_start(out=u_sb[:, 4 * g : 4 * g + 4, :], in_=uv[g])
         for i, s in enumerate((wx_scales, v1_scales, wh_scales)):
             for q in range(4):
-                nc.sync.dma_start(
+                nc.gpsimd.dma_start(
                     out=ws[32 * q : 32 * q + 8, i, :].bitcast(I32), in_=s[:, 4 * q : 4 * q + 4, :].bitcast(I32)
                 )
         for i, w in ((0, wx_words), (2, wh_words), (1, v1_words)):
@@ -139,15 +144,16 @@ def tile_grownetnewtontargets_x2_kernel(
                 )
             else:
                 nc.scalar.activation(out=out, in_=acc[:], func=ACT.Relu, accum_out=sums[:, ht, g : g + 1])
-            if g == 1:
-                nc.gpsimd.tensor_scalar(
-                    out=mean[:, ht : ht + 1],
-                    in0=sums[:, ht, 0:1],
-                    scalar1=sums[:, ht, 1:2],
-                    scalar2=1.0 / B,
-                    op0=ALU.add,
-                    op1=ALU.mult,
-                )
+
+        def average(ht):
+            nc.vector.tensor_scalar(
+                out=mean[:, ht : ht + 1],
+                in0=sums[:, ht, 0:1],
+                scalar1=sums[:, ht, 1:2],
+                scalar2=1.0 / B,
+                op0=ALU.add,
+                op1=ALU.mult,
+            )
 
         def centre(eng, ht):
             gh, t = ht // 4, ht % 4
@@ -161,7 +167,7 @@ def tile_grownetnewtontargets_x2_kernel(
                     op1=ALU.mult,
                 )
             else:
-                nc.gpsimd.tensor_scalar(
+                nc.vector.tensor_scalar(
                     out=nmg[:, ht : ht + 1],
                     in0=mean[:, ht : ht + 1],
                     scalar1=-1.0,
@@ -178,11 +184,12 @@ def tile_grownetnewtontargets_x2_kernel(
                 )
 
         def interleave(eng, gh, g, lo=0, hi=512):
-            src = hc[:, gh, :, 512 * g + lo : 512 * g + hi].rearrange("p t n -> p n t")
+            src = hc[:, gh, :, 512 * g + lo : 512 * g + hi].rearrange("p t (n i) -> p n t i", i=4)
+            out = hg[:, gh, g, lo:hi, :].rearrange("p (n i) t -> p n t i", i=4)
             if eng == "v":
-                nc.vector.tensor_copy(out=hg[:, gh, g, lo:hi, :], in_=src)
+                nc.vector.tensor_copy(out=out, in_=src)
             else:
-                nc.scalar.copy(out=hg[:, gh, g, lo:hi, :], in_=src)
+                nc.scalar.copy(out=out, in_=src)
 
         def quant_h(gh, g):
             nc.vector.quantize_mx(
@@ -259,11 +266,12 @@ def tile_grownetnewtontargets_x2_kernel(
                 nc.sync.dma_start(out=o0v[g][:, t, :], in_=o[:, g, t, :])
 
         def weave(eng, g, lo, hi):
-            src = o[:, g, :, lo:hi].rearrange("p t c -> p c t")
+            src = o[:, g, :, lo:hi].rearrange("p t (c i) -> p c t i", i=4)
+            out = pb[:, g, lo:hi, :].rearrange("p (c i) t -> p c t i", i=4)
             if eng == "v":
-                nc.vector.tensor_copy(out=pb[:, g, lo:hi, :], in_=src)
+                nc.vector.tensor_copy(out=out, in_=src)
             else:
-                nc.scalar.copy(out=pb[:, g, lo:hi, :], in_=src)
+                nc.scalar.copy(out=out, in_=src)
 
         def planes(g):
             nc.vector.quantize_mx(
@@ -271,21 +279,29 @@ def tile_grownetnewtontargets_x2_kernel(
             )
             nc.sync.dma_start(out=out_1[g].rearrange("p m t -> p (m t)").bitcast(I32), in_=pq[:, g, :])
             for qd in range(4):
-                nc.sync.dma_start(
+                (nc.sync if g == 0 else nc.scalar).dma_start(
                     out=out_2[g][4 * qd : 4 * qd + 4, :].bitcast(I32), in_=ps[g][32 * qd : 32 * qd + 4, :].bitcast(I32)
                 )
 
+        def spin(dst, n):
+            nc.tensor.matmul(out=dst[:, 0:n], lhsT=blank[:, 0:P], rhs=blank[:, 0:n], start=True, stop=True)
+
+        idle = psum.tile([P, 512], F32, name="bank")
+        for i in range(7):
+            spin(idle, 512)
+        for j in range(4):
+            lay("s", j, turn(j))
+            spin(idle, 384)
+            if j == 1:
+                quant_x(0, 0)
         nc.vector.tensor_copy(
             out=w1sp[:].rearrange("p (g t) m -> p g t m", g=2), in_=w1s[:].rearrange("p (g m t) -> p g t m", g=2, t=4)
         )
-        for j in range(4):
-            lay("s", j, turn(j))
-            if j == 1:
-                quant_x(0, 0)
         order_w1(0)
         quant_x(0, 1)
         for j in range(4, 8):
             lay("s", j, turn(j))
+            spin(idle, 384)
             if j == 5:
                 quant_x(1, 0)
         quant_x(1, 1)
@@ -297,12 +313,17 @@ def tile_grownetnewtontargets_x2_kernel(
         signs(1)
         for ht in range(4):
             stage1("s", ht, 1)
+        average(0)
+        average(1)
         centre("v", 0)
+        average(2)
         centre("v", 1)
+        average(3)
         centre("v", 2)
         stage1("s", 4, 0)
         stage1("v", 4, 1)
         centre("v", 3)
+        average(4)
         stage1("s", 5, 0)
         stage1("s", 5, 1)
         interleave("v", 0, 0)
@@ -311,10 +332,13 @@ def tile_grownetnewtontargets_x2_kernel(
         stage1("s", 6, 1)
         stage1("s", 7, 0)
         stage1("s", 7, 1)
-        centre("v", 5)
+        average(5)
         centre("s", 4)
-        centre("v", 6)
+        average(6)
+        centre("v", 5)
+        average(7)
         centre("s", 7)
+        centre("v", 6)
         interleave("v", 0, 1, 256, 512)
         interleave("v", 1, 0, 0, 320)
         interleave("s", 1, 0, 320, 512)
@@ -325,6 +349,9 @@ def tile_grownetnewtontargets_x2_kernel(
         interleave("s", 1, 1, 0, 256)
         for j in range(6):
             open_p(j)
+        idle2 = psum.tile([P, 512], F32, name="bank")
+        for i in range(6):
+            spin(idle2, 512)
         for j in range(4):
             close_p(j)
             open_s(j)
@@ -344,6 +371,7 @@ def tile_grownetnewtontargets_x2_kernel(
                     open_s(i)
             if j >= 2:
                 if j == 9:
+                    planes(0)
                     final(7, 0, 256)
                     final(7, 256, 512)
                 else:
@@ -356,6 +384,5 @@ def tile_grownetnewtontargets_x2_kernel(
             if j == 8:
                 weave("v", 0, 384, 512)
         weave("s", 1, 0, 192)
-        planes(0)
         weave("v", 1, 192, 512)
         planes(1)

@@ -45,11 +45,11 @@ def tile_grownetnewtontargets_x2_kernel(
         ln2 = keep.tile([P, 1], F32, name="ln2")
         warm = keep.tile([P, 1], F32, name="warm")
         sums = keep.tile([P, 8, 2], F32, name="sums", align_bytes=64)
-        mean = keep.tile([P, 8], F32, name="mean", align_bytes=64)
         nmg = keep.tile([P, 8], F32, name="nmg", align_bytes=64)
+        mean = keep.tile([P, 8], F32, name="mean", align_bytes=64)
         r = keep.tile([P, 8, 1024], F32, name="r", align_bytes=64)
-        hc = keep.tile([P, 2, 4, 1024], BF16, name="hc", align_bytes=64)
-        hg = keep.tile([P, 2, 2, 512, 4], BF16, name="hg", align_bytes=64)
+        hc = keep.tile([P, 2, 2, 2048], BF16, name="hc", align_bytes=64)
+        hg = keep.tile([P, 2, 2, 2048], BF16, name="hg", align_bytes=64)
         hq = keep.tile([P, 2, 1024], I32, name="hq", align_bytes=64)
         hs = keep.tile([P, 2, 1024], U8, name="hs", align_bytes=64)
         o = keep.tile([P, 2, 4, 512], F32, name="o", align_bytes=64)
@@ -60,9 +60,9 @@ def tile_grownetnewtontargets_x2_kernel(
         ps = [ps0, ps1]
 
         ctx.enter_context(tc.manual_schedule())
-        nc.vector.memset(w1s[:].bitcast(I32), 0)
         blank = keep.tile([P, 512], BF16, name="blank", align_bytes=64)
         nc.vector.memset(blank[:], 0.0)
+        nc.vector.memset(w1s[:].bitcast(I32), 0)
         nc.vector.memset(zero[:], 0.0)
         nc.vector.memset(ws[:].rearrange("p w n -> p (w n)").bitcast(I32), 0)
         make_identity(nc, ident[:])
@@ -74,18 +74,19 @@ def tile_grownetnewtontargets_x2_kernel(
         nc.scalar.activation(out=warm[:], in_=zero[:], func=ACT.Exp)
         nc.gpsimd.dma_start(out=g1b[:], in_=g1.rearrange("(g p t) -> p g t", p=P, t=4))
         nc.sync.dma_start(out=x_sb[:, 0, :], in_=xv[0][:, 0, :])
+        nc.sync.dma_start(out=x_sb[:, 1, :], in_=xv[0][:, 1, :])
+        nc.sync.dma_start(out=x_sb[:, 2:4, :], in_=xv[0][:, 2:4, :])
         for q in range(4):
             nc.sync.dma_start(
                 out=w1s[32 * q : 32 * q + 8, :].bitcast(I32), in_=w1_scales[:, 4 * q : 4 * q + 4, :].bitcast(I32)
             )
-        nc.sync.dma_start(out=x_sb[:, 1, :], in_=xv[0][:, 1, :])
-        nc.sync.dma_start(out=x_sb[:, 2:4, :], in_=xv[0][:, 2:4, :])
         nc.sync.dma_start(out=w1w[:, 0, :, :], in_=w1v[:, :, 0:512])
         nc.sync.dma_start(out=x_sb[:, 4:6, :], in_=xv[1][:, 0:2, :])
-        nc.sync.dma_start(out=x_sb[:, 6:8, :], in_=xv[1][:, 2:4, :])
-        nc.sync.dma_start(out=w1w[:, 1, :, :], in_=w1v[:, :, 512:1024])
+        nc.sync.dma_start(out=x_sb[:, 6, :], in_=xv[1][:, 2, :])
+        nc.sync.dma_start(out=x_sb[:, 7, :], in_=xv[1][:, 3, :])
         for g in range(2):
             nc.sync.dma_start(out=u_sb[:, 4 * g : 4 * g + 4, :], in_=uv[g])
+        nc.sync.dma_start(out=w1w[:, 1, :, :], in_=w1v[:, :, 512:1024])
         for i, s in enumerate((wx_scales, v1_scales, wh_scales)):
             for q in range(4):
                 nc.gpsimd.dma_start(
@@ -111,13 +112,12 @@ def tile_grownetnewtontargets_x2_kernel(
             else:
                 nc.scalar.copy(out=out, in_=src)
 
-        def quant_x(g, half):
+        def quant_x(g, lo, hi):
             for k in range(2):
-                c = slice(512 * g + 256 * half, 512 * g + 256 * half + 256)
                 nc.vector.quantize_mx(
-                    out=xq[:, k, c].bitcast(FP8X4),
-                    scales=xs[:, k, c],
-                    in_=xg[:, g, k, 256 * half : 256 * half + 256, :].rearrange("p n t -> p (n t)"),
+                    out=xq[:, k, 512 * g + lo : 512 * g + hi].bitcast(FP8X4),
+                    scales=xs[:, k, 512 * g + lo : 512 * g + hi],
+                    in_=xg[:, g, k, lo:hi, :].rearrange("p n t -> p (n t)"),
                 )
 
         def order_w1(gh):
@@ -155,37 +155,36 @@ def tile_grownetnewtontargets_x2_kernel(
                 op1=ALU.mult,
             )
 
-        def centre(eng, ht):
+        def centre(eng, ht, lo=0, hi=1024):
             gh, t = ht // 4, ht % 4
+            out = hc[:, gh, t // 2, :].rearrange("p (b e) -> p b e", e=2)[:, lo:hi, t % 2]
             if eng == "v":
                 nc.vector.tensor_scalar(
-                    out=hc[:, gh, t, :],
-                    in0=r[:, ht, :],
+                    out=out,
+                    in0=r[:, ht, lo:hi],
                     scalar1=mean[:, ht : ht + 1],
                     scalar2=g1f[:, ht : ht + 1],
                     op0=ALU.subtract,
                     op1=ALU.mult,
                 )
             else:
-                nc.vector.tensor_scalar(
-                    out=nmg[:, ht : ht + 1],
-                    in0=mean[:, ht : ht + 1],
-                    scalar1=-1.0,
-                    scalar2=g1f[:, ht : ht + 1],
-                    op0=ALU.mult,
-                    op1=ALU.mult,
-                )
                 nc.scalar.activation(
-                    out=hc[:, gh, t, :],
-                    in_=r[:, ht, :],
-                    func=ACT.Identity,
-                    scale=g1f[:, ht : ht + 1],
-                    bias=nmg[:, ht : ht + 1],
+                    out=out, in_=r[:, ht, lo:hi], func=ACT.Identity, scale=g1f[:, ht : ht + 1], bias=nmg[:, ht : ht + 1]
                 )
 
+        def shift(ht):
+            nc.vector.tensor_scalar(
+                out=nmg[:, ht : ht + 1],
+                in0=mean[:, ht : ht + 1],
+                scalar1=-1.0,
+                scalar2=g1f[:, ht : ht + 1],
+                op0=ALU.mult,
+                op1=ALU.mult,
+            )
+
         def interleave(eng, gh, g, lo=0, hi=512):
-            src = hc[:, gh, :, 512 * g + lo : 512 * g + hi].rearrange("p t (n i) -> p n t i", i=4)
-            out = hg[:, gh, g, lo:hi, :].rearrange("p (n i) t -> p n t i", i=4)
+            src = hc[:, gh, :, 1024 * g + 2 * lo : 1024 * g + 2 * hi].bitcast(F32).rearrange("p a n -> p n a")
+            out = hg[:, gh, g, 4 * lo : 4 * hi].bitcast(F32).rearrange("p (n a) -> p n a", a=2)
             if eng == "v":
                 nc.vector.tensor_copy(out=out, in_=src)
             else:
@@ -195,7 +194,7 @@ def tile_grownetnewtontargets_x2_kernel(
             nc.vector.quantize_mx(
                 out=hq[:, gh, 512 * g : 512 * g + 512].bitcast(FP8X4),
                 scales=hs[:, gh, 512 * g : 512 * g + 512],
-                in_=hg[:, gh, g, :, :].rearrange("p n t -> p (n t)"),
+                in_=hg[:, gh, g, :],
             )
 
         def signs(g):
@@ -287,66 +286,52 @@ def tile_grownetnewtontargets_x2_kernel(
             nc.tensor.matmul(out=dst[:, 0:n], lhsT=blank[:, 0:P], rhs=blank[:, 0:n], start=True, stop=True)
 
         idle = psum.tile([P, 512], F32, name="bank")
-        for i in range(7):
+        for i in range(4):
             spin(idle, 512)
         for j in range(4):
             lay("s", j, turn(j))
             spin(idle, 384)
-            if j == 1:
-                quant_x(0, 0)
         nc.vector.tensor_copy(
             out=w1sp[:].rearrange("p (g t) m -> p g t m", g=2), in_=w1s[:].rearrange("p (g m t) -> p g t m", g=2, t=4)
         )
+        quant_x(0, 0, 512)
         order_w1(0)
-        quant_x(0, 1)
         for j in range(4, 8):
-            lay("s", j, turn(j))
+            lay("v" if j % 2 else "s", j, turn(j))
             spin(idle, 384)
             if j == 5:
-                quant_x(1, 0)
-        quant_x(1, 1)
+                quant_x(1, 0, 256)
+        quant_x(1, 256, 512)
         for ht in range(4):
             stage1("v" if ht == 2 else "s", ht, 0)
-        order_w1(1)
         nc.vector.tensor_copy(out=g1f[:], in_=g1b[:].rearrange("p g t -> p (g t)"))
         signs(0)
         signs(1)
+        order_w1(1)
         for ht in range(4):
             stage1("s", ht, 1)
         average(0)
-        average(1)
-        centre("v", 0)
-        average(2)
-        centre("v", 1)
-        average(3)
-        centre("v", 2)
-        stage1("s", 4, 0)
-        stage1("v", 4, 1)
-        centre("v", 3)
-        average(4)
-        stage1("s", 5, 0)
-        stage1("s", 5, 1)
-        interleave("v", 0, 0)
-        quant_h(0, 0)
-        stage1("v", 6, 0)
-        stage1("s", 6, 1)
+        for ht in range(6):
+            if ht >= 3:
+                stage1("v" if ht == 4 else "s", ht + 1, 0)
+                stage1("s", ht + 1, 1)
+            average(ht + 1)
+            centre("v", ht)
         stage1("s", 7, 0)
         stage1("s", 7, 1)
-        average(5)
-        centre("s", 4)
-        average(6)
-        centre("v", 5)
         average(7)
-        centre("s", 7)
-        centre("v", 6)
-        interleave("v", 0, 1, 256, 512)
-        interleave("v", 1, 0, 0, 320)
-        interleave("s", 1, 0, 320, 512)
+        shift(6)
+        shift(7)
+        interleave("s", 0, 0)
+        for ht in (6, 7):
+            centre("v", ht, 0, 512)
+            centre("s", ht, 512, 1024)
+        interleave("v", 1, 0)
+        quant_h(0, 0)
         quant_h(1, 0)
-        interleave("s", 0, 1, 0, 256)
+        interleave("s", 0, 1)
         quant_h(0, 1)
-        interleave("v", 1, 1, 256, 512)
-        interleave("s", 1, 1, 0, 256)
+        interleave("s", 1, 1)
         for j in range(6):
             open_p(j)
         idle2 = psum.tile([P, 512], F32, name="bank")
@@ -358,9 +343,8 @@ def tile_grownetnewtontargets_x2_kernel(
             if j in (1, 2):
                 open_p(j + 5)
         tanh(0)
-        tanh(1)
         for j in range(10):
-            if 1 <= j < 7:
+            if j < 7:
                 tanh(j + 1)
             if j < 8:
                 add(j)
@@ -369,20 +353,16 @@ def tile_grownetnewtontargets_x2_kernel(
                 for i in range(4, 8):
                     close_p(i)
                     open_s(i)
-            if j >= 2:
-                if j == 9:
-                    planes(0)
-                    final(7, 0, 256)
-                    final(7, 256, 512)
-                else:
-                    final(j - 2)
+            if 2 <= j < 9:
+                final(j - 2)
             if j < 8:
                 sign(j)
                 expo(j)
-            if 5 <= j < 8:
+            if 5 <= j < 9:
                 weave("s", 0, 128 * (j - 5), 128 * (j - 4))
-            if j == 8:
-                weave("v", 0, 384, 512)
-        weave("s", 1, 0, 192)
-        weave("v", 1, 192, 512)
+        final(7, 0, 256)
+        weave("s", 1, 0, 224)
+        final(7, 256, 512)
+        planes(0)
+        weave("v", 1, 224, 512)
         planes(1)

@@ -87,13 +87,13 @@ def tile_grownetnewtontargets_x2_kernel(
         for g in range(2):
             nc.sync.dma_start(out=u_sb[:, 4 * g : 4 * g + 4, :], in_=uv[g])
         nc.sync.dma_start(out=w1w[:, 1, :, :], in_=w1v[:, :, 512:1024])
-        for i, s in enumerate((wx_scales, v1_scales, wh_scales)):
-            for q in range(4):
-                nc.gpsimd.dma_start(
-                    out=ws[32 * q : 32 * q + 8, i, :].bitcast(I32), in_=s[:, 4 * q : 4 * q + 4, :].bitcast(I32)
-                )
         for i, w in ((0, wx_words), (2, wh_words), (1, v1_words)):
             nc.sync.dma_start(out=ww[:, i, :, :], in_=w.rearrange("g p n t -> p g (n t)").bitcast(I32))
+        for i, s in ((0, wx_scales), (2, wh_scales), (1, v1_scales)):
+            for q in range(4):
+                nc.sync.dma_start(
+                    out=ws[32 * q : 32 * q + 8, i, :].bitcast(I32), in_=s[:, 4 * q : 4 * q + 4, :].bitcast(I32)
+                )
 
         def turn(j):
             xw = x_sb[:, j, :].bitcast(F32)
@@ -261,8 +261,7 @@ def tile_grownetnewtontargets_x2_kernel(
             nc.vector.scalar_tensor_tensor(
                 out=o[:, g, t, lo:hi], in0=e2s[j][:, lo:hi], scalar=2.0, in1=hy[:, j, lo:hi], op0=ALU.add, op1=ALU.mult
             )
-            if hi == 512:
-                nc.sync.dma_start(out=o0v[g][:, t, :], in_=o[:, g, t, :])
+            nc.sync.dma_start(out=o0v[g][:, t, lo:hi], in_=o[:, g, t, lo:hi])
 
         def weave(eng, g, lo, hi):
             src = o[:, g, :, lo:hi].rearrange("p t (c i) -> p c t i", i=4)
@@ -291,19 +290,23 @@ def tile_grownetnewtontargets_x2_kernel(
         for j in range(4):
             lay("s", j, turn(j))
             spin(idle, 384)
+            if j == 1:
+                quant_x(0, 0, 256)
         nc.vector.tensor_copy(
             out=w1sp[:].rearrange("p (g t) m -> p g t m", g=2), in_=w1s[:].rearrange("p (g m t) -> p g t m", g=2, t=4)
         )
-        quant_x(0, 0, 512)
         order_w1(0)
-        for j in range(4, 8):
-            lay("v" if j % 2 else "s", j, turn(j))
-            spin(idle, 384)
-            if j == 5:
-                quant_x(1, 0, 256)
+        quant_x(0, 256, 512)
+        lay("s", 4, turn(4))
+        lay("v", 5, turn(5))
+        quant_x(1, 0, 256)
+        stage1("s", 0, 0)
+        lay("s", 6, turn(6))
+        lay("v", 7, turn(7))
         quant_x(1, 256, 512)
-        for ht in range(4):
-            stage1("v" if ht == 2 else "s", ht, 0)
+        stage1("s", 1, 0)
+        stage1("s", 2, 0)
+        stage1("s", 3, 0)
         nc.vector.tensor_copy(out=g1f[:], in_=g1b[:].rearrange("p g t -> p (g t)"))
         signs(0)
         signs(1)
@@ -313,7 +316,7 @@ def tile_grownetnewtontargets_x2_kernel(
         average(0)
         for ht in range(6):
             if ht >= 3:
-                stage1("v" if ht == 4 else "s", ht + 1, 0)
+                stage1("s", ht + 1, 0)
                 stage1("s", ht + 1, 1)
             average(ht + 1)
             centre("v", ht)
@@ -358,11 +361,14 @@ def tile_grownetnewtontargets_x2_kernel(
             if j < 8:
                 sign(j)
                 expo(j)
-            if 5 <= j < 9:
+            if 5 <= j < 8:
                 weave("s", 0, 128 * (j - 5), 128 * (j - 4))
+            if j == 7:
+                weave("v", 0, 384, 512)
+            if j == 8:
+                planes(0)
         final(7, 0, 256)
         weave("s", 1, 0, 224)
         final(7, 256, 512)
-        planes(0)
         weave("v", 1, 224, 512)
         planes(1)

@@ -197,10 +197,10 @@ def tile_grownetnewtontargets_x2_kernel(
                 in_=hg[:, gh, g, :],
             )
 
-        def signs(g):
+        def signs():
             nc.vector.tensor_scalar(
-                out=hy[:, 4 * g : 4 * g + 4, :],
-                in0=u_sb[:, 4 * g : 4 * g + 4, :],
+                out=hy[:],
+                in0=u_sb[:],
                 scalar1=0.0,
                 scalar2=0.5,
                 op0=ALU.is_ge,
@@ -261,7 +261,8 @@ def tile_grownetnewtontargets_x2_kernel(
             nc.vector.scalar_tensor_tensor(
                 out=o[:, g, t, lo:hi], in0=e2s[j][:, lo:hi], scalar=2.0, in1=hy[:, j, lo:hi], op0=ALU.add, op1=ALU.mult
             )
-            nc.sync.dma_start(out=o0v[g][:, t, lo:hi], in_=o[:, g, t, lo:hi])
+            if hi == 512:
+                nc.sync.dma_start(out=o0v[g][:, t, :], in_=o[:, g, t, :])
 
         def weave(eng, g, lo, hi):
             src = o[:, g, :, lo:hi].rearrange("p t (c i) -> p c t i", i=4)
@@ -277,7 +278,7 @@ def tile_grownetnewtontargets_x2_kernel(
             )
             nc.sync.dma_start(out=out_1[g].rearrange("p m t -> p (m t)").bitcast(I32), in_=pq[:, g, :])
             for qd in range(4):
-                (nc.sync if g == 0 else nc.scalar).dma_start(
+                (nc.sync if g == 0 or qd >= 2 else nc.scalar).dma_start(
                     out=out_2[g][4 * qd : 4 * qd + 4, :].bitcast(I32), in_=ps[g][32 * qd : 32 * qd + 4, :].bitcast(I32)
                 )
 
@@ -308,8 +309,7 @@ def tile_grownetnewtontargets_x2_kernel(
         stage1("s", 2, 0)
         stage1("s", 3, 0)
         nc.vector.tensor_copy(out=g1f[:], in_=g1b[:].rearrange("p g t -> p (g t)"))
-        signs(0)
-        signs(1)
+        signs()
         order_w1(1)
         for ht in range(4):
             stage1("s", ht, 1)
@@ -332,7 +332,7 @@ def tile_grownetnewtontargets_x2_kernel(
         interleave("v", 1, 0)
         quant_h(0, 0)
         quant_h(1, 0)
-        interleave("s", 0, 1)
+        interleave("v", 0, 1)
         quant_h(0, 1)
         interleave("s", 1, 1)
         for j in range(6):
@@ -349,6 +349,8 @@ def tile_grownetnewtontargets_x2_kernel(
         for j in range(10):
             if j < 7:
                 tanh(j + 1)
+            if j in (6, 7):
+                weave("s", 0, 128 * (j - 6), 128 * (j - 5))
             if j < 8:
                 add(j)
             if j == 1:
@@ -361,14 +363,12 @@ def tile_grownetnewtontargets_x2_kernel(
             if j < 8:
                 sign(j)
                 expo(j)
-            if 5 <= j < 8:
-                weave("s", 0, 128 * (j - 5), 128 * (j - 4))
             if j == 7:
-                weave("v", 0, 384, 512)
+                weave("v", 0, 256, 512)
             if j == 8:
                 planes(0)
         final(7, 0, 256)
-        weave("s", 1, 0, 224)
+        weave("s", 1, 0, 192)
         final(7, 256, 512)
-        weave("v", 1, 224, 512)
+        weave("v", 1, 192, 512)
         planes(1)

from contextlib import ExitStack

import concourse.mybir as mybir
from concourse.masks import make_identity

F32 = mybir.dt.float32
BF16 = mybir.dt.bfloat16
I32 = mybir.dt.int32
U8 = mybir.dt.uint8
FP8X4 = mybir.dt.float8_e4m3fn_x4
ALU = mybir.AluOpType
ACT = mybir.ActivationFunctionType

B, D, H, C = 1024, 1024, 1024, 512
P = 128
FLOPS = 2 * B * D * H + 3 * 2 * B * D * C
LN2 = 0.6931471805599453


def tile_grownetnewtontargets_x2_kernel(
    tc, x, w1_words, w1_scales, g1, v1_words, v1_scales, wx_words, wx_scales, wh_words, wh_scales, u, out_0, out_1, out_2
):
    nc = tc.nc
    with ExitStack() as ctx:
        keep = ctx.enter_context(tc.tile_pool(name="keep", bufs=1))
        work = ctx.enter_context(tc.tile_pool(name="work", bufs=4))
        psum = ctx.enter_context(tc.psum_pool(name="psum", bufs=8))

        ident = keep.tile([P, P], F32, name="ident")
        w1s = keep.tile([P, 1024], U8, name="w1s", align_bytes=64)
        w1sp = keep.tile([P, 8, 128], U8, name="w1sp", align_bytes=64)
        ws = keep.tile([P, 3, 512], U8, name="ws", align_bytes=64)
        x_sb = keep.tile([P, 8, 1024], BF16, name="x_sb", align_bytes=64)
        xg = keep.tile([P, 2, 2, 512, 4], BF16, name="xg", align_bytes=64)
        xq = keep.tile([P, 2, 1024], I32, name="xq", align_bytes=64)
        xs = keep.tile([P, 2, 1024], U8, name="xs", align_bytes=64)
        w1w = keep.tile([P, 2, 2, 512], I32, name="w1w", align_bytes=64)
        w1p = keep.tile([P, 2, 8, 128], I32, name="w1p", align_bytes=64)
        ww = keep.tile([P, 3, 2, 512], I32, name="ww", align_bytes=64)
        u_sb = keep.tile([P, 8, 512], BF16, name="u_sb", align_bytes=64)
        hy = keep.tile([P, 8, 512], BF16, name="hy", align_bytes=64)
        g1b = keep.tile([P, 2, 4], BF16, name="g1b", align_bytes=64)
        g1f = keep.tile([P, 8], F32, name="g1f", align_bytes=64)
        zero = keep.tile([P, 1], F32, name="zero")
        ln2 = keep.tile([P, 1], F32, name="ln2")
        warm = keep.tile([P, 1], F32, name="warm")
        sums = keep.tile([P, 8, 2], F32, name="sums", align_bytes=64)
        nmg = keep.tile([P, 8], F32, name="nmg", align_bytes=64)
        mean = keep.tile([P, 8], F32, name="mean", align_bytes=64)
        r = keep.tile([P, 8, 1024], F32, name="r", align_bytes=64)
        hc = keep.tile([P, 2, 2, 2048], BF16, name="hc", align_bytes=64)
        hg = keep.tile([P, 2, 2, 2048], BF16, name="hg", align_bytes=64)
        hq = keep.tile([P, 2, 1024], I32, name="hq", align_bytes=64)
        hs = keep.tile([P, 2, 1024], U8, name="hs", align_bytes=64)
        o = keep.tile([P, 2, 4, 512], F32, name="o", align_bytes=64)
        pb = keep.tile([P, 2, 512, 4], BF16, name="pb", align_bytes=64)
        pq = keep.tile([P, 2, 512], I32, name="pq", align_bytes=64)
        ps0 = keep.tile([P, 512], U8, name="ps0", align_bytes=64)
        ps1 = keep.tile([P, 512], U8, name="ps1", align_bytes=64)
        ps = [ps0, ps1]

        ctx.enter_context(tc.manual_schedule())
        blank = keep.tile([P, 512], BF16, name="blank", align_bytes=64)
        nc.vector.memset(blank[:], 0.0)
        nc.vector.memset(w1s[:].bitcast(I32), 0)
        nc.vector.memset(zero[:], 0.0)
        nc.vector.memset(ws[:].rearrange("p w n -> p (w n)").bitcast(I32), 0)
        make_identity(nc, ident[:])
        nc.vector.tensor_scalar(out=ln2[:], in0=zero[:], scalar1=1.0, scalar2=LN2, op0=ALU.mult, op1=ALU.add)

        xv = x.rearrange("(g p t) k -> g p t k", p=P, t=4)
        w1v = w1_words.rearrange("g p n t -> p g (n t)").bitcast(I32)
        uv = u.rearrange("(g p t) c -> g p t c", p=P, t=4)
        nc.scalar.activation(out=warm[:], in_=zero[:], func=ACT.Exp)
        nc.gpsimd.dma_start(out=g1b[:], in_=g1.rearrange("(g p t) -> p g t", p=P, t=4))
        nc.sync.dma_start(out=x_sb[:, 0, :], in_=xv[0][:, 0, :])
        nc.sync.dma_start(out=x_sb[:, 1, :], in_=xv[0][:, 1, :])
        nc.sync.dma_start(out=x_sb[:, 2:4, :], in_=xv[0][:, 2:4, :])
        for q in range(4):
            nc.sync.dma_start(
                out=w1s[32 * q : 32 * q + 8, :].bitcast(I32), in_=w1_scales[:, 4 * q : 4 * q + 4, :].bitcast(I32)
            )
        nc.sync.dma_start(out=w1w[:, 0, :, :], in_=w1v[:, :, 0:512])
        nc.sync.dma_start(out=x_sb[:, 4:6, :], in_=xv[1][:, 0:2, :])
        nc.sync.dma_start(out=x_sb[:, 6, :], in_=xv[1][:, 2, :])
        nc.sync.dma_start(out=x_sb[:, 7, :], in_=xv[1][:, 3, :])
        for g in range(2):
            nc.sync.dma_start(out=u_sb[:, 4 * g : 4 * g + 4, :], in_=uv[g])
        nc.sync.dma_start(out=w1w[:, 1, :, :], in_=w1v[:, :, 512:1024])
        for i, w in ((0, wx_words), (2, wh_words), (1, v1_words)):
            nc.sync.dma_start(out=ww[:, i, :, :], in_=w.rearrange("g p n t -> p g (n t)").bitcast(I32))
        for i, s in ((0, wx_scales), (2, wh_scales), (1, v1_scales)):
            for q in range(4):
                nc.sync.dma_start(
                    out=ws[32 * q : 32 * q + 8, i, :].bitcast(I32), in_=s[:, 4 * q : 4 * q + 4, :].bitcast(I32)
                )

        def turn(j):
            xw = x_sb[:, j, :].bitcast(F32)
            xt = psum.tile([P, 4, P], F32, name="bank")
            for k in range(2):
                for e in range(2):
                    nc.tensor.transpose(xt[:, 2 * k + e, :], xw[:, 256 * k + e : 256 * (k + 1) : 2], ident[:])
            return xt

        def lay(eng, j, xt):
            g, t = j // 4, j % 4
            out = xg[:, g, :, 128 * t : 128 * t + 128, :].bitcast(F32)
            src = xt[:].rearrange("p (k e) n -> p k n e", k=2)
            if eng == "v":
                nc.vector.tensor_copy(out=out, in_=src)
            else:
                nc.scalar.copy(out=out, in_=src)

        def quant_x(g, lo, hi):
            for k in range(2):
                nc.vector.quantize_mx(
                    out=xq[:, k, 512 * g + lo : 512 * g + hi].bitcast(FP8X4),
                    scales=xs[:, k, 512 * g + lo : 512 * g + hi],
                    in_=xg[:, g, k, lo:hi, :].rearrange("p n t -> p (n t)"),
                )

        def order_w1(gh):
            nc.vector.tensor_copy(
                out=w1p[:, :, 4 * gh : 4 * gh + 4, :], in_=w1w[:, gh, :, :].rearrange("p k (m t) -> p k t m", t=4)
            )

        def stage1(eng, ht, g):
            acc = psum.tile([P, 512], F32, name="bank")
            for k in range(2):
                nc.tensor.matmul_mx(
                    out=acc[:],
                    lhsT=w1p[:, k, ht, :].bitcast(FP8X4),
                    lhsT_scale=w1sp[4 * k :, ht, :],
                    rhs=xq[:, k, 512 * g : 512 * g + 512].bitcast(FP8X4),
                    rhs_scale=xs[:, k, 512 * g : 512 * g + 512],
                    start=(k == 0),
                    stop=(k == 1),
                )
            out = r[:, ht, 512 * g : 512 * g + 512]
            if eng == "v":
                nc.vector.tensor_scalar(
                    out=out, in0=acc[:], scalar1=0.0, scalar2=None, op0=ALU.max, op1=ALU.add, accum_out=sums[:, ht, g : g + 1]
                )
            else:
                nc.scalar.activation(out=out, in_=acc[:], func=ACT.Relu, accum_out=sums[:, ht, g : g + 1])

        def average(ht):
            nc.vector.tensor_scalar(
                out=mean[:, ht : ht + 1],
                in0=sums[:, ht, 0:1],
                scalar1=sums[:, ht, 1:2],
                scalar2=1.0 / B,
                op0=ALU.add,
                op1=ALU.mult,
            )

        def centre(eng, ht, lo=0, hi=1024):
            gh, t = ht // 4, ht % 4
            out = hc[:, gh, t // 2, :].rearrange("p (b e) -> p b e", e=2)[:, lo:hi, t % 2]
            if eng == "v":
                nc.vector.tensor_scalar(
                    out=out,
                    in0=r[:, ht, lo:hi],
                    scalar1=mean[:, ht : ht + 1],
                    scalar2=g1f[:, ht : ht + 1],
                    op0=ALU.subtract,
                    op1=ALU.mult,
                )
            else:
                nc.scalar.activation(
                    out=out, in_=r[:, ht, lo:hi], func=ACT.Identity, scale=g1f[:, ht : ht + 1], bias=nmg[:, ht : ht + 1]
                )

        def shift(ht):
            nc.vector.tensor_scalar(
                out=nmg[:, ht : ht + 1],
                in0=mean[:, ht : ht + 1],
                scalar1=-1.0,
                scalar2=g1f[:, ht : ht + 1],
                op0=ALU.mult,
                op1=ALU.mult,
            )

        def interleave(eng, gh, g, lo=0, hi=512):
            src = hc[:, gh, :, 1024 * g + 2 * lo : 1024 * g + 2 * hi].bitcast(F32).rearrange("p a n -> p n a")
            out = hg[:, gh, g, 4 * lo : 4 * hi].bitcast(F32).rearrange("p (n a) -> p n a", a=2)
            if eng == "v":
                nc.vector.tensor_copy(out=out, in_=src)
            else:
                nc.scalar.copy(out=out, in_=src)

        def quant_h(gh, g):
            nc.vector.quantize_mx(
                out=hq[:, gh, 512 * g : 512 * g + 512].bitcast(FP8X4),
                scales=hs[:, gh, 512 * g : 512 * g + 512],
                in_=hg[:, gh, g, :],
            )

        def signs():
            nc.vector.tensor_scalar(
                out=hy[:],
                in0=u_sb[:],
                scalar1=0.0,
                scalar2=0.5,
                op0=ALU.is_ge,
                op1=ALU.subtract,
            )

        def passes(acc, codes, scales, j, wi, first, last):
            for k in range(2):
                nc.tensor.matmul_mx(
                    out=acc[:],
                    lhsT=codes[:, k, P * j : P * j + P].bitcast(FP8X4),
                    lhsT_scale=scales[:, k, P * j : P * j + P],
                    rhs=ww[:, wi, k, :].bitcast(FP8X4),
                    rhs_scale=ws[4 * k :, wi, :],
                    start=(first and k == 0),
                    stop=(last and k == 1),
                )

        pbank, sbank, ths, qs, e1s, e2s = {}, {}, {}, {}, {}, {}

        def open_p(j):
            acc = psum.tile([P, 512], F32, name="bank")
            passes(acc, xq, xs, j, 0, True, False)
            pbank[j] = acc

        def close_p(j):
            passes(pbank[j], hq, hs, j, 2, False, True)

        def open_s(j):
            acc = psum.tile([P, 512], F32, name="bank")
            passes(acc, hq, hs, j, 1, True, True)
            sbank[j] = acc

        def tanh(j):
            th = work.tile([P, 512], F32, name="th")
            nc.scalar.activation(out=th[:], in_=pbank[j][:], func=ACT.Tanh)
            ths[j] = th

        def add(j):
            q = work.tile([P, 512], F32, name="q")
            nc.vector.tensor_tensor(out=q[:], in0=sbank[j][:], in1=ths[j][:], op=ALU.add)
            qs[j] = q

        def sign(j):
            e1 = work.tile([P, 512], F32, name="e1")
            nc.vector.tensor_tensor(out=e1[:], in0=qs[j][:], in1=hy[:, j, :], op=ALU.mult)
            e1s[j] = e1

        def expo(j):
            e2 = work.tile([P, 512], F32, name="e2")
            nc.scalar.activation(out=e2[:], in_=e1s[j][:], func=ACT.Exp, bias=ln2[:], scale=-1.6)
            e2s[j] = e2

        o0v = out_0.rearrange("(g p t) c -> g p t c", p=P, t=4)

        def final(j, lo=0, hi=512):
            g, t = j // 4, j % 4
            nc.vector.scalar_tensor_tensor(
                out=o[:, g, t, lo:hi], in0=e2s[j][:, lo:hi], scalar=2.0, in1=hy[:, j, lo:hi], op0=ALU.add, op1=ALU.mult
            )
            if hi == 512:
                nc.sync.dma_start(out=o0v[g][:, t, :], in_=o[:, g, t, :])

        def weave(eng, g, lo, hi):
            src = o[:, g, :, lo:hi].rearrange("p t (c i) -> p c t i", i=4)
            out = pb[:, g, lo:hi, :].rearrange("p (c i) t -> p c t i", i=4)
            if eng == "v":
                nc.vector.tensor_copy(out=out, in_=src)
            else:
                nc.scalar.copy(out=out, in_=src)

        def planes(g):
            nc.vector.quantize_mx(
                out=pq[:, g, :].bitcast(FP8X4), scales=ps[g][:], in_=pb[:, g, :, :].rearrange("p c t -> p (c t)")
            )
            nc.sync.dma_start(out=out_1[g].rearrange("p m t -> p (m t)").bitcast(I32), in_=pq[:, g, :])
            for qd in range(4):
                (nc.sync if g == 0 or qd >= 2 else nc.scalar).dma_start(
                    out=out_2[g][4 * qd : 4 * qd + 4, :].bitcast(I32), in_=ps[g][32 * qd : 32 * qd + 4, :].bitcast(I32)
                )

        def spin(dst, n):
            nc.tensor.matmul(out=dst[:, 0:n], lhsT=blank[:, 0:P], rhs=blank[:, 0:n], start=True, stop=True)

        idle = psum.tile([P, 512], F32, name="bank")
        for i in range(4):
            spin(idle, 512)
        for j in range(4):
            lay("s", j, turn(j))
            spin(idle, 384)
            if j == 1:
                quant_x(0, 0, 256)
        nc.vector.tensor_copy(
            out=w1sp[:].rearrange("p (g t) m -> p g t m", g=2), in_=w1s[:].rearrange("p (g m t) -> p g t m", g=2, t=4)
        )
        order_w1(0)
        quant_x(0, 256, 512)
        lay("s", 4, turn(4))
        lay("v", 5, turn(5))
        quant_x(1, 0, 256)
        stage1("s", 0, 0)
        lay("s", 6, turn(6))
        lay("v", 7, turn(7))
        quant_x(1, 256, 512)
        stage1("s", 1, 0)
        stage1("s", 2, 0)
        stage1("s", 3, 0)
        nc.vector.tensor_copy(out=g1f[:], in_=g1b[:].rearrange("p g t -> p (g t)"))
        signs()
        order_w1(1)
        for ht in range(4):
            stage1("s", ht, 1)
        average(0)
        for ht in range(6):
            if ht >= 3:
                stage1("s", ht + 1, 0)
                stage1("s", ht + 1, 1)
            average(ht + 1)
            centre("v", ht)
        stage1("s", 7, 0)
        stage1("s", 7, 1)
        average(7)
        shift(6)
        shift(7)
        interleave("s", 0, 0)
        for ht in (6, 7):
            centre("v", ht, 0, 512)
            centre("s", ht, 512, 1024)
        interleave("v", 1, 0)
        quant_h(0, 0)
        quant_h(1, 0)
        interleave("v", 0, 1)
        quant_h(0, 1)
        interleave("s", 1, 1)
        for j in range(6):
            open_p(j)
        idle2 = psum.tile([P, 512], F32, name="bank")
        for i in range(6):
            spin(idle2, 512)
        for j in range(4):
            close_p(j)
            open_s(j)
            if j in (1, 2):
                open_p(j + 5)
        tanh(0)
        for j in range(10):
            if j < 7:
                tanh(j + 1)
            if j in (6, 7):
                weave("s", 0, 128 * (j - 6), 128 * (j - 5))
            if j < 8:
                add(j)
            if j == 1:
                quant_h(1, 1)
                for i in range(4, 8):
                    close_p(i)
                    open_s(i)
            if 2 <= j < 9:
                final(j - 2)
            if j < 8:
                sign(j)
                expo(j)
            if j == 7:
                weave("v", 0, 256, 512)
            if j == 8:
                planes(0)
        final(7, 0, 256)
        weave("s", 1, 0, 192)
        final(7, 256, 512)
        weave("v", 1, 192, 512)
        planes(1)
